import numpy as np
import ml_dtypes


def mxq(x, axis, fmt="e4m3"):
    dtype, down = {"e4m3": (ml_dtypes.float8_e4m3fn, 7), "e5m2": (ml_dtypes.float8_e5m2, 14)}[fmt]
    v = np.moveaxis(np.asarray(x, np.float32).astype(ml_dtypes.bfloat16).astype(np.float64), axis, -1)
    blocks = v.reshape(v.shape[:-1] + (-1, 32))
    amax = np.abs(blocks).max(-1, keepdims=True)
    byte = np.maximum(np.where(amax > 0, np.frexp(amax)[1] - 1 + 127, 0) - down, 1)
    scale = np.exp2(byte - 127.0)
    codes = (blocks / scale).astype(np.float32).astype(dtype).astype(np.float64)
    return np.moveaxis((codes * scale).reshape(v.shape), -1, axis)


WIDE = False


def mx_kscale(k):
    if not WIDE:
        return np.ones(k)
    levels = np.array([10, -10, 5, -5, 0])
    if k % 512:
        return np.exp2(np.random.permutation(np.resize(levels, k // 32))).repeat(32)
    a = np.empty((k // 512, 16))
    for p in range(k // 512):
        a[p, :8] = np.random.permutation(np.resize(levels, 8))
        for g in range(8):
            far = levels[np.abs(levels - a[p, g]) >= 10]
            a[p, g + 8] = far[np.random.randint(len(far))]
    return np.exp2(a.ravel()).repeat(32)


def f64(x):
    return np.asarray(x).astype(np.float64)


def striped(idx):
    return np.tile(idx.reshape(-1, 16).T, (8, 1)).astype(np.uint16)


def unstriped(offs):
    return offs[:16].T.reshape(-1).astype(np.int64)


def pack_weight(w):
    k, n = w.shape
    w = f64(np.asarray(w, np.float32).astype(ml_dtypes.bfloat16)).reshape(k // 32, 32, n)
    amax = np.abs(w).max(1)
    byte = np.clip(np.where(amax > 0, np.frexp(amax)[1] - 1 + 127 - 7, 1), 1, 254)
    scaled = (w * np.exp2(127.0 - byte)[:, None, :]).reshape(k, n).astype(np.float32)
    words = np.ascontiguousarray(scaled.reshape(k // 512, 128, 4, n).transpose(0, 1, 3, 2)).astype(ml_dtypes.float8_e4m3fn).view(np.uint8)
    return words, np.ascontiguousarray(byte.astype(np.uint8).reshape(k // 512, 16, n))


def unpack_weight(words, scales):
    g, p, n, _ = words.shape
    vals = np.ascontiguousarray(words).view(ml_dtypes.float8_e4m3fn).astype(np.float64) * np.repeat(np.exp2(scales.astype(np.float64) - 127.0), 8, axis=1)[..., None]
    return vals.transpose(0, 1, 3, 2).reshape(g * 512, n)


E2M1 = np.array([0.0, 0.5, 1.0, 1.5, 2.0, 3.0, 4.0, 6.0, -0.0, -0.5, -1.0, -1.5, -2.0, -3.0, -4.0, -6.0])


def pack_fp4(w):
    k, n = w.shape
    w = f64(np.asarray(w, np.float32).astype(ml_dtypes.bfloat16)).reshape(k // 32, 32, n)
    amax = np.abs(w).max(1)
    mant, ex = np.frexp(amax / 6.0)
    byte = np.clip(np.where(amax > 0, np.where(mant > 0.5, ex, ex - 1) + 127, 1), 1, 254)
    scaled = (w * np.exp2(127.0 - byte)[:, None, :]).reshape(k, n).astype(np.float32)
    c = np.ascontiguousarray(scaled.reshape(k // 512, 128, 4, n).transpose(0, 1, 3, 2)).astype(ml_dtypes.float4_e2m1fn).view(np.uint8) & 0xF
    words = (c[..., 0::2] | (c[..., 1::2] << 4)).reshape(k // 512, 128, 2 * n)
    return np.ascontiguousarray(words), np.ascontiguousarray(byte.astype(np.uint8).reshape(k // 512, 16, n))


def unpack_fp4(words, scales):
    g, _, n = scales.shape
    words = np.ascontiguousarray(words).reshape(g, 128, n, 2)
    nib = np.empty((g, 128, n, 4), np.uint8)
    nib[..., 0::2] = words & 0xF
    nib[..., 1::2] = words >> 4
    vals = E2M1[nib] * np.repeat(np.exp2(scales.astype(np.float64) - 127.0), 8, axis=1)[..., None]
    return vals.transpose(0, 1, 3, 2).reshape(g * 512, n)


def sigmoid(v):
    return 1.0 / (1.0 + np.exp(-np.maximum(v, -700.0)))


K, T, S, D, N, H, V, U = 512, 4096, 1024, 4, 256, 512, 256, 512


def setup_inputs():
    n = np.random.standard_normal
    s = mx_kscale(K)[:, None]
    u = mx_kscale(H)
    packed_xT = pack_weight(n((K, T)) * s)
    packed_w1 = pack_fp4(n((K, H)) / np.sqrt(K) / s)
    packed_w2 = pack_fp4(n((K, H)) / np.sqrt(K) / s)
    packed_w3 = pack_fp4(n((H, N)) / np.sqrt(H) / u[:, None])
    return {
        "x_words": packed_xT[0],
        "x_scales": packed_xT[1],
        "w1_words": packed_w1[0],
        "w1_scales": packed_w1[1],
        "w2_words": packed_w2[0],
        "w2_scales": packed_w2[1],
        "conc": (np.random.uniform(0.3, 1.5, (H, S))).astype(np.float32),
        "unit": (np.random.uniform(0.6, 1.4, (H, 1)) * u[:, None]).astype(np.float32),
        "w3_words": packed_w3[0],
        "w3_scales": packed_w3[1],
        "offs": striped(np.random.permutation(T)[:S]),
        "cof": striped(np.random.permutation(S)),
        "gene": striped(np.random.permutation(np.concatenate([np.arange(V), np.random.randint(0, V, U - V)]))),
    }


def reference(x_words, x_scales, w1_words, w1_scales, w2_words, w2_scales, conc, unit, w3_words, w3_scales, offs, cof, gene):
    xq = unpack_weight(x_words, x_scales)[:, unstriped(offs)]
    y = unpack_fp4(w1_words, w1_scales).T @ xq
    kd = np.exp(1.0 * np.tanh(y))
    zz1 = unpack_fp4(w2_words, w2_scales).T @ xq
    zc = zz1[:, unstriped(cof)]
    coop = 1.5 * sigmoid(zc) + 0.5
    wt = (kd * coop) * f64(conc)
    part = wt.reshape(len(wt), -1, D).sum(axis=2) + 1.0
    occ = wt / np.repeat(part, D, axis=1)
    act = occ * zz1
    drv = act.reshape(len(act), -1, D).sum(axis=2)
    pg = drv[:, unstriped(gene)]
    hid = f64(unit) * (sigmoid(2.0 * pg) * part[:, unstriped(gene)])
    return unpack_fp4(w3_words, w3_scales).T @ mxq(hid, 0, "e4m3")

@@ -1,0 +1,227 @@
+from contextlib import ExitStack
+
+import concourse.mybir as mybir
+from concourse.masks import make_identity
+
+K, T, S, D, N, H, V, U = 512, 4096, 1024, 4, 256, 512, 256, 512
+FLOPS = 2 * K * H * S * 2 + 2 * H * N * U
+
+F32 = mybir.dt.float32
+BF16 = mybir.dt.bfloat16
+I32 = mybir.dt.int32
+U32 = mybir.dt.uint32
+U16 = mybir.dt.uint16
+U8 = mybir.dt.uint8
+FP8X4 = mybir.dt.float8_e4m3fn_x4
+FP4X4 = mybir.dt.float4_e2m1fn_x4
+ACT = mybir.ActivationFunctionType
+ALU = mybir.AluOpType
+
+P = 128
+PACK = 4
+HALF = 512
+LIST_COLS = HALF // 16
+GH = U // 2
+
+
+def load_scale_rows(queue, plane, scales, quads=range(4)):
+    for quad in quads:
+        queue.dma_start(
+            out=plane[32 * quad : 32 * quad + 4, :].bitcast(I32),
+            in_=scales[0, 4 * quad : 4 * quad + 4, :].bitcast(I32),
+        )
+
+
+def tile_picked_ytfcmp_sig_p_kernel(
+    tc, x_words, x_scales, w1_words, w1_scales, w2_words, w2_scales, conc, unit, w3_words, w3_scales, offs, cof, gene, out
+):
+    nc = tc.nc
+    with ExitStack() as ctx:
+        keep = ctx.enter_context(tc.tile_pool(name="keep", bufs=1))
+        work = ctx.enter_context(tc.tile_pool(name="work", bufs=2))
+        psum = ctx.enter_context(tc.psum_pool(name="psum", bufs=1))
+
+        offs_t = keep.tile([P, S // 16], U16, name="offs_t")
+        cof_t = keep.tile([P, S // 16], U16, name="cof_t")
+        gene_t = keep.tile([P, U // 16], U16, name="gene_t")
+
+        x_tab = keep.tile([P, T], U32, name="x_tab", align_bytes=64)
+        xs_tab = keep.tile([P, T], U8, name="xs_tab", align_bytes=64)
+        w_raw = [keep.tile([P, 2 * H], U8, name="w_raw%d" % i, align_bytes=64) for i in range(2)]
+        ws_raw = [keep.tile([P, H], U8, name="ws_raw%d" % i, align_bytes=64) for i in range(2)]
+        w_deal = [keep.tile([P, 2 * H], U8, name="w_deal%d" % i, align_bytes=64) for i in range(2)]
+        ws_deal = [keep.tile([P, H], U8, name="ws_deal%d" % i, align_bytes=64) for i in range(2)]
+        w3_t = keep.tile([P, 2 * N], U8, name="w3_t", align_bytes=64)
+        w3s_t = keep.tile([P, N], U8, name="w3s_t", align_bytes=64)
+        conc_t = [keep.tile([P, S], F32, name="conc%d" % t) for t in range(PACK)]
+        unit_t = keep.tile([P, PACK], F32, name="unit_t")
+        ident = keep.tile([P, P], F32, name="ident")
+        enh = [keep.tile([P, 2 * V], F32, name="enh%d" % t) for t in range(PACK)]
+        hid_planes = [keep.tile([P, PACK, GH], BF16, name="hid_planes%d" % g, align_bytes=64) for g in range(2)]
+
+        nc.vector.memset(xs_tab[:].bitcast(I32), 0)
+        for i in range(2):
+            nc.gpsimd.memset(ws_raw[i][:].bitcast(I32), 0)
+        nc.sync.dma_start(offs_t[:], offs)
+        load_scale_rows(nc.scalar, xs_tab, x_scales)
+        nc.sync.dma_start(out=w_raw[0][:].bitcast(I32), in_=w2_words[0].bitcast(I32))
+        nc.sync.dma_start(out=w_raw[1][:].bitcast(I32), in_=w1_words[0].bitcast(I32))
+        load_scale_rows(nc.sync, ws_raw[0], w2_scales, range(1))
+        nc.sync.dma_start(out=x_tab[:].bitcast(I32), in_=x_words[0].rearrange("p n t -> p (n t)").bitcast(I32))
+        load_scale_rows(nc.scalar, ws_raw[0], w2_scales, range(1, 4))
+        load_scale_rows(nc.gpsimd, ws_raw[1], w1_scales)
+        nc.sync.dma_start(cof_t[:], cof)
+        conc_rows = conc.rearrange("(p t) s -> p t s", t=PACK)
+        for t in range(PACK):
+            nc.sync.dma_start(out=conc_t[t][:], in_=conc_rows[:, t, :])
+        nc.sync.dma_start(gene_t[:], gene)
+        nc.sync.dma_start(out=unit_t[:], in_=unit.rearrange("(p t) o -> p (t o)", t=PACK))
+        nc.sync.dma_start(out=w3_t[:].bitcast(I32), in_=w3_words[0].bitcast(I32))
+        nc.gpsimd.memset(w3s_t[:].bitcast(I32), 0)
+        load_scale_rows(nc.sync, w3s_t, w3_scales)
+
+        for i, eng in enumerate((nc.vector, nc.gpsimd)):
+            eng.tensor_copy(
+                out=w_deal[i][:].rearrange("p (t m b) -> p t m b", t=PACK, b=2),
+                in_=w_raw[i][:].rearrange("p (m t b) -> p t m b", t=PACK, b=2),
+            )
+        xw = [keep.tile([P, HALF], U32, name="xw%d" % h, align_bytes=64) for h in range(2)]
+        xs = [keep.tile([P, HALF], U8, name="xs%d" % h, align_bytes=64) for h in range(2)]
+        for h in range(2):
+            nc.vector.tensor_copy(xs[h][:], xs_tab[:].indirect(offs_t[:, h * LIST_COLS : (h + 1) * LIST_COLS]))
+        for i, eng in enumerate((nc.vector, nc.gpsimd)):
+            eng.tensor_copy(
+                out=ws_deal[i][:].rearrange("p (t m) -> p t m", t=PACK),
+                in_=ws_raw[i][:].rearrange("p (m t) -> p t m", t=PACK),
+            )
+        for h in range(2):
+            nc.vector.tensor_copy(xw[h][:], x_tab[:].indirect(offs_t[:, h * LIST_COLS : (h + 1) * LIST_COLS]))
+
+        make_identity(nc, ident[:])
+        for t in range(PACK):
+            nc.gpsimd.memset(enh[t][:, V:], 0.0)
+
+        def product(acc, i, t, h):
+            nc.tensor.matmul_mx(
+                out=acc[:],
+                lhsT=w_deal[i][:, 2 * P * t : 2 * P * (t + 1)].bitcast(FP4X4),
+                lhsT_scale=ws_deal[i][:, P * t : P * (t + 1)],
+                rhs=xw[h][:].bitcast(FP8X4),
+                rhs_scale=xs[h][:],
+                start=True,
+                stop=True,
+            )
+
+        def paired(ap):
+            return ap.rearrange("p (v e b) -> p e v b", e=2, b=2)
+
+        def as_pairs(ap):
+            return ap.rearrange("p (e v b) -> p e v b", e=2, b=2)
+
+        def group_sums(acc, values, first):
+            members = first + [values[:, e * 256 + b : (e + 1) * 256 : 2] for e in range(2) for b in range(2)]
+            for n, member in enumerate(members):
+                nc.tensor.matmul(acc, member, ident[:], start=(n == 0), stop=(n == len(members) - 1), is_transpose=True)
+
+        for t in range(PACK):
+            z = [psum.tile([P, HALF], F32, name="z%d" % h, tag="z", bufs=4) for h in range(2)]
+            y = [psum.tile([P, HALF], F32, name="y%d" % h, tag="y", bufs=2) for h in range(2)]
+            tz = work.tile([P, S], F32, name="tz", tag="tz%d" % (t % 2), bufs=1)
+            kc = []
+            tc_ = []
+            for h in range(2):
+                product(z[h], 0, t, h)
+                product(y[h], 1, t, h)
+                nc.scalar.activation(tz[:, h * HALF : (h + 1) * HALF], z[h][:], ACT.Tanh, scale=0.5)
+            for h in range(2):
+                th = work.tile([P, HALF], F32, name="th", tag="th", bufs=2)
+                nc.scalar.activation(as_pairs(th[:]), paired(y[h][:]), ACT.Tanh)
+                kd = work.tile([P, HALF], F32, name="kd", tag="kd", bufs=2)
+                nc.scalar.activation(kd[:], th[:], ACT.Exp)
+                kc_h = work.tile([P, HALF], F32, name="kc_h", tag="kc_h", bufs=4)
+                (nc.vector if (t, h) in ((0,0),(0,1)) else nc.gpsimd).tensor_tensor(
+                    as_pairs(kc_h[:]), paired(conc_t[t][:, h * HALF : (h + 1) * HALF]), as_pairs(kd[:]), ALU.mult
+                )
+                kc.append(kc_h)
+            for h in range(2):
+                picked = work.tile([P, HALF], F32, name="picked", tag="picked", bufs=4)
+                window = tz[:].indirect(cof_t[:, h * LIST_COLS : (h + 1) * LIST_COLS])
+                if (t, h) in ((0,0),(0,1),(3,0)):
+                    nc.vector.tensor_copy(picked[:], window)
+                else:
+                    nc.scalar.activation(picked[:], window, ACT.Copy, bias=5.0 / 3.0)
+                tc_.append(picked)
+            part = psum.tile([P, V], F32, name="part", tag="part", bufs=1)
+            part_sb = work.tile([P, V], F32, name="part_sb")
+            wt = []
+            for h in range(2):
+                wt_h = work.tile([P, HALF], F32, name="wt_h", tag="wt_h", bufs=4)
+                if (t, h) in ((0,0),(0,1),(3,0)):
+                    for e in range(2):
+                        nc.vector.scalar_tensor_tensor(
+                            as_pairs(wt_h[:])[:, e], paired(tc_[h][:])[:, e], 5.0 / 3.0, as_pairs(kc[h][:])[:, e], ALU.add, ALU.mult
+                        )
+                else:
+                    nc.vector.tensor_tensor(as_pairs(wt_h[:]), paired(tc_[h][:]), as_pairs(kc[h][:]), ALU.mult)
+                wt.append(wt_h)
+                group_sums(part[:, h * P : (h + 1) * P], wt_h, [])
+                nc.scalar.activation(part_sb[:, h * P : (h + 1) * P], part[:, h * P : (h + 1) * P], ACT.Copy, scale=0.375, bias=0.5)
+            part_back = psum.tile([P, V], F32, name="part_back", tag="part", bufs=1)
+            for h in range(2):
+                nc.tensor.transpose(part_back[:, h * P : (h + 1) * P], part_sb[:, h * P : (h + 1) * P], ident[:])
+            pu = work.tile([P, V], F32, name="pu")
+            nc.scalar.activation(pu[:], part_back[:], ACT.Copy, scale=unit_t[:, t : t + 1])
+            num = psum.tile([P, V], F32, name="num", tag="num", bufs=1)
+            for h in range(2):
+                wz = work.tile([P, HALF], F32, name="wz", tag="wz", bufs=2)
+                nc.vector.tensor_tensor(as_pairs(wz[:]), paired(z[h][:]), as_pairs(wt[h][:]), ALU.mult)
+                group_sums(num[:, h * P : (h + 1) * P], wz, [])
+            inv = work.tile([P, V], F32, name="inv")
+            for h in range(2):
+                nc.vector.reciprocal(inv[:, h * P : (h + 1) * P], part_sb[:, h * P : (h + 1) * P])
+            drv = work.tile([P, V], F32, name="drv")
+            nc.vector.tensor_tensor(drv[:], num[:], inv[:], ALU.mult)
+            back = psum.tile([P, V], F32, name="back", tag="num", bufs=1)
+            for h in range(2):
+                nc.tensor.transpose(back[:, h * P : (h + 1) * P], drv[:, h * P : (h + 1) * P], ident[:])
+            td = work.tile([P, V], F32, name="td")
+            nc.scalar.activation(td[:], back[:], ACT.Tanh, scale=0.375)
+            nc.vector.scalar_tensor_tensor(enh[t][:, :V], td[:], 1.0, pu[:], ALU.add, ALU.mult)
+            if t < PACK - 1:
+                for g in range(2):
+                    window = enh[t][:].indirect(gene_t[:, g * (GH // 16) : (g + 1) * (GH // 16)])
+                    nc.scalar.activation(hid_planes[g][:, t, :], window, ACT.Copy)
+
+        groups = []
+        for g in range(2):
+            grouped = work.tile([P, GH, PACK], BF16, name="grouped", align_bytes=64)
+            nc.vector.tensor_copy(
+                out=grouped[:, :, : PACK - 1].rearrange("p (c i) t -> p c t i", i=4),
+                in_=hid_planes[g][:, : PACK - 1, :].rearrange("p t (c i) -> p c t i", i=4),
+            )
+            groups.append(grouped)
+        for g in range(2):
+            grouped = groups[g]
+            nc.vector.tensor_copy(
+                grouped[:, :, PACK - 1], enh[PACK - 1][:].indirect(gene_t[:, g * (GH // 16) : (g + 1) * (GH // 16)])
+            )
+            codes = work.tile([P, GH], U32, name="codes", align_bytes=64)
+            scales = work.tile([P, GH], U8, name="scales", align_bytes=64)
+            nc.vector.quantize_mx(out=codes[:].bitcast(FP8X4), scales=scales[:], in_=grouped[:].rearrange("p r t -> p (r t)"))
+            for m in range(N // P):
+                acc = psum.tile([P, GH], F32, name="acc", tag="z", bufs=4)
+                nc.tensor.matmul_mx(
+                    out=acc[:],
+                    lhsT=w3_t[:, 2 * P * m : 2 * P * (m + 1)].bitcast(FP4X4),
+                    lhsT_scale=w3s_t[:, P * m : P * (m + 1)],
+                    rhs=codes[:].bitcast(FP8X4),
+                    rhs_scale=scales[:],
+                    start=True,
+                    stop=True,
+                )
+                res = work.tile([P, GH], F32, name="res", tag="res", bufs=4)
+                if g == 1 and m == 1:
+                    nc.vector.tensor_copy(res[:], acc[:])
+                else:
+                    nc.scalar.copy(res[:], acc[:])
+                nc.sync.dma_start(out=out[m * P : (m + 1) * P, g * GH : (g + 1) * GH], in_=res[:])

@@ -22,6 +22,7 @@ PACK = 4
 HALF = 512
 LIST_COLS = HALF // 16
 GH = U // 2
+SHRINK = 2.0**-48
 
 
 def load_scale_rows(queue, plane, scales, quads=range(4)):
@@ -56,6 +57,7 @@ def tile_picked_ytfcmp_sig_p_kernel(
         conc_t = [keep.tile([P, S], F32, name="conc%d" % t) for t in range(PACK)]
         unit_t = keep.tile([P, PACK], F32, name="unit_t")
         ident = keep.tile([P, P], F32, name="ident")
+        unit_s = keep.tile([P, PACK], F32, name="unit_s")
         enh = [keep.tile([P, 2 * V], F32, name="enh%d" % t) for t in range(PACK)]
         hid_planes = [keep.tile([P, PACK, GH], BF16, name="hid_planes%d" % g, align_bytes=64) for g in range(2)]
 
@@ -69,8 +71,8 @@ def tile_picked_ytfcmp_sig_p_kernel(
         load_scale_rows(nc.sync, ws_raw[0], w2_scales, range(1))
         nc.sync.dma_start(out=x_tab[:].bitcast(I32), in_=x_words[0].rearrange("p n t -> p (n t)").bitcast(I32))
         load_scale_rows(nc.scalar, ws_raw[0], w2_scales, range(1, 4))
-        load_scale_rows(nc.gpsimd, ws_raw[1], w1_scales)
         nc.sync.dma_start(cof_t[:], cof)
+        load_scale_rows(nc.sync, ws_raw[1], w1_scales)
         conc_rows = conc.rearrange("(p t) s -> p t s", t=PACK)
         for t in range(PACK):
             nc.sync.dma_start(out=conc_t[t][:], in_=conc_rows[:, t, :])
@@ -80,7 +82,7 @@ def tile_picked_ytfcmp_sig_p_kernel(
         nc.gpsimd.memset(w3s_t[:].bitcast(I32), 0)
         load_scale_rows(nc.sync, w3s_t, w3_scales)
 
-        for i, eng in enumerate((nc.vector, nc.gpsimd)):
+        for i, eng in enumerate((nc.vector, nc.vector)):
             eng.tensor_copy(
                 out=w_deal[i][:].rearrange("p (t m b) -> p t m b", t=PACK, b=2),
                 in_=w_raw[i][:].rearrange("p (m t b) -> p t m b", t=PACK, b=2),
@@ -89,7 +91,7 @@ def tile_picked_ytfcmp_sig_p_kernel(
         xs = [keep.tile([P, HALF], U8, name="xs%d" % h, align_bytes=64) for h in range(2)]
         for h in range(2):
             nc.vector.tensor_copy(xs[h][:], xs_tab[:].indirect(offs_t[:, h * LIST_COLS : (h + 1) * LIST_COLS]))
-        for i, eng in enumerate((nc.vector, nc.gpsimd)):
+        for i, eng in enumerate((nc.vector, nc.vector)):
             eng.tensor_copy(
                 out=ws_deal[i][:].rearrange("p (t m) -> p t m", t=PACK),
                 in_=ws_raw[i][:].rearrange("p (m t) -> p t m", t=PACK),
@@ -98,8 +100,7 @@ def tile_picked_ytfcmp_sig_p_kernel(
             nc.vector.tensor_copy(xw[h][:], x_tab[:].indirect(offs_t[:, h * LIST_COLS : (h + 1) * LIST_COLS]))
 
         make_identity(nc, ident[:])
-        for t in range(PACK):
-            nc.gpsimd.memset(enh[t][:, V:], 0.0)
+        nc.gpsimd.tensor_scalar(unit_s[:], unit_t[:], 1.0 / SHRINK, 0.0, ALU.mult, ALU.add)
 
         def product(acc, i, t, h):
             nc.tensor.matmul_mx(
@@ -123,87 +124,107 @@ def tile_picked_ytfcmp_sig_p_kernel(
             for n, member in enumerate(members):
                 nc.tensor.matmul(acc, member, ident[:], start=(n == 0), stop=(n == len(members) - 1), is_transpose=True)
 
-        for t in range(PACK):
+        def front(t):
             z = [psum.tile([P, HALF], F32, name="z%d" % h, tag="z", bufs=4) for h in range(2)]
             y = [psum.tile([P, HALF], F32, name="y%d" % h, tag="y", bufs=2) for h in range(2)]
             tz = work.tile([P, S], F32, name="tz", tag="tz%d" % (t % 2), bufs=1)
-            kc = []
-            tc_ = []
+            kd, picked = [], []
             for h in range(2):
                 product(z[h], 0, t, h)
                 product(y[h], 1, t, h)
                 nc.scalar.activation(tz[:, h * HALF : (h + 1) * HALF], z[h][:], ACT.Tanh, scale=0.5)
             for h in range(2):
+                pick = work.tile([P, HALF], F32, name="pick", tag="pick", bufs=6)
+                window = tz[:].indirect(cof_t[:, h * LIST_COLS : (h + 1) * LIST_COLS])
+                if (t, h) in ((0,0),(0,1)):
+                    nc.vector.tensor_copy(pick[:], window)
+                else:
+                    nc.scalar.activation(pick[:], window, ACT.Copy)
+                picked.append(pick)
+            for h in range(2):
                 th = work.tile([P, HALF], F32, name="th", tag="th", bufs=2)
                 nc.scalar.activation(as_pairs(th[:]), paired(y[h][:]), ACT.Tanh)
-                kd = work.tile([P, HALF], F32, name="kd", tag="kd", bufs=2)
-                nc.scalar.activation(kd[:], th[:], ACT.Exp)
-                kc_h = work.tile([P, HALF], F32, name="kc_h", tag="kc_h", bufs=4)
-                (nc.vector if (t, h) in ((0,0),(0,1)) else nc.gpsimd).tensor_tensor(
-                    as_pairs(kc_h[:]), paired(conc_t[t][:, h * HALF : (h + 1) * HALF]), as_pairs(kd[:]), ALU.mult
-                )
-                kc.append(kc_h)
-            for h in range(2):
-                picked = work.tile([P, HALF], F32, name="picked", tag="picked", bufs=4)
-                window = tz[:].indirect(cof_t[:, h * LIST_COLS : (h + 1) * LIST_COLS])
-                if (t, h) in ((0,0),(0,1),(3,0)):
-                    nc.vector.tensor_copy(picked[:], window)
-                else:
-                    nc.scalar.activation(picked[:], window, ACT.Copy, bias=5.0 / 3.0)
-                tc_.append(picked)
+                kd_h = work.tile([P, HALF], F32, name="kd_h", tag="kd_h", bufs=6)
+                nc.scalar.activation(kd_h[:], th[:], ACT.Exp)
+                kd.append(kd_h)
+            return z, kd, picked
+
+        def middle(t, z, kd, picked, late):
             part = psum.tile([P, V], F32, name="part", tag="part", bufs=1)
-            part_sb = work.tile([P, V], F32, name="part_sb")
             wt = []
             for h in range(2):
+                cc = work.tile([P, HALF], F32, name="cc", tag="cc", bufs=2)
+                nc.vector.scalar_tensor_tensor(
+                    cc[:], picked[h][:], 5.0 / 3.0, conc_t[t][:, h * HALF : (h + 1) * HALF], ALU.add, ALU.mult
+                )
                 wt_h = work.tile([P, HALF], F32, name="wt_h", tag="wt_h", bufs=4)
-                if (t, h) in ((0,0),(0,1),(3,0)):
-                    for e in range(2):
-                        nc.vector.scalar_tensor_tensor(
-                            as_pairs(wt_h[:])[:, e], paired(tc_[h][:])[:, e], 5.0 / 3.0, as_pairs(kc[h][:])[:, e], ALU.add, ALU.mult
-                        )
-                else:
-                    nc.vector.tensor_tensor(as_pairs(wt_h[:]), paired(tc_[h][:]), as_pairs(kc[h][:]), ALU.mult)
+                nc.vector.tensor_tensor(as_pairs(wt_h[:]), paired(cc[:]), as_pairs(kd[h][:]), ALU.mult)
                 wt.append(wt_h)
                 group_sums(part[:, h * P : (h + 1) * P], wt_h, [])
-                nc.scalar.activation(part_sb[:, h * P : (h + 1) * P], part[:, h * P : (h + 1) * P], ACT.Copy, scale=0.375, bias=0.5)
-            part_back = psum.tile([P, V], F32, name="part_back", tag="part", bufs=1)
-            for h in range(2):
-                nc.tensor.transpose(part_back[:, h * P : (h + 1) * P], part_sb[:, h * P : (h + 1) * P], ident[:])
-            pu = work.tile([P, V], F32, name="pu")
-            nc.scalar.activation(pu[:], part_back[:], ACT.Copy, scale=unit_t[:, t : t + 1])
             num = psum.tile([P, V], F32, name="num", tag="num", bufs=1)
             for h in range(2):
                 wz = work.tile([P, HALF], F32, name="wz", tag="wz", bufs=2)
                 nc.vector.tensor_tensor(as_pairs(wz[:]), paired(z[h][:]), as_pairs(wt[h][:]), ALU.mult)
-                group_sums(num[:, h * P : (h + 1) * P], wz, [])
-            inv = work.tile([P, V], F32, name="inv")
-            for h in range(2):
-                nc.vector.reciprocal(inv[:, h * P : (h + 1) * P], part_sb[:, h * P : (h + 1) * P])
-            drv = work.tile([P, V], F32, name="drv")
-            nc.vector.tensor_tensor(drv[:], num[:], inv[:], ALU.mult)
-            back = psum.tile([P, V], F32, name="back", tag="num", bufs=1)
-            for h in range(2):
-                nc.tensor.transpose(back[:, h * P : (h + 1) * P], drv[:, h * P : (h + 1) * P], ident[:])
+                group_sums(num[:, (1 - h) * P : (2 - h) * P], wz, [])
+            part_sb = enh[t][:, V:]
+            nc.vector.tensor_scalar(part_sb, part[:], 0.375 * SHRINK, 0.5 * SHRINK, ALU.mult, ALU.add)
+            prod = work.tile([P, 1, P], F32, name="prod")
+            nc.vector.tensor_tensor(prod[:, 0, :], part_sb[:, :P], part_sb[:, P:], ALU.mult)
+            if late:
+                finish(*late)
+            inv = work.tile([P, 1, P], F32, name="inv")
+            nc.vector.reciprocal(inv[:], prod[:])
+            cross = work.tile([P, V], F32, name="cross")
+            nc.vector.tensor_tensor(cross[:], num[:], part_sb, ALU.mult)
+            drv = work.tile([P, 2, P], F32, name="drv")
+            nc.vector.tensor_tensor(
+                drv[:], cross[:].rearrange("p (h v) -> p h v", h=2), inv[:].to_broadcast([P, 2, P]), ALU.mult
+            )
+            if t == PACK - 1:
+                pu = work.tile([P, V], F32, name="pu")
+                turn(pu[:], [part_sb[:, h * P : (h + 1) * P] for h in range(2)], "part", ACT.Copy, unit_s[:, t : t + 1])
+                td = work.tile([P, V], F32, name="td")
+                turn(td[:], [drv[:, 1 - h, :] for h in range(2)], "num", ACT.Tanh, 0.375 * SHRINK)
+                nc.vector.scalar_tensor_tensor(enh[t][:, :V], td[:], 1.0, pu[:], ALU.add, ALU.mult)
+                return None
             td = work.tile([P, V], F32, name="td")
-            nc.scalar.activation(td[:], back[:], ACT.Tanh, scale=0.375)
-            nc.vector.scalar_tensor_tensor(enh[t][:, :V], td[:], 1.0, pu[:], ALU.add, ALU.mult)
-            if t < PACK - 1:
-                for g in range(2):
-                    window = enh[t][:].indirect(gene_t[:, g * (GH // 16) : (g + 1) * (GH // 16)])
+            for h in range(2):
+                nc.scalar.activation(td[:, h * P : (h + 1) * P], drv[:, 1 - h, :], ACT.Tanh, scale=0.375 * SHRINK)
+            return t, td
+
+        def turn(dst, halves, tag, func, scale):
+            back = psum.tile([P, V], F32, name="back", tag=tag, bufs=1)
+            for h in range(2):
+                nc.tensor.transpose(back[:, h * P : (h + 1) * P], halves[h], ident[:])
+            nc.scalar.activation(dst, back[:], func, scale=scale)
+
+        def finish(t, td):
+            ft = work.tile([P, V], F32, name="ft")
+            nc.vector.scalar_tensor_tensor(ft[:], td[:], 1.0, enh[t][:, V:], ALU.add, ALU.mult)
+            turn(enh[t][:, :V], [ft[:, h * P : (h + 1) * P] for h in range(2)], "part", ACT.Copy, unit_s[:, t : t + 1])
+            look_up_genes(t)
+
+        def look_up_genes(t):
+            for g in range(2):
+                window = enh[t][:].indirect(gene_t[:, g * (GH // 16) : (g + 1) * (GH // 16)])
+                if t == PACK - 1 and g == 0:
+                    nc.vector.tensor_copy(hid_planes[g][:, t, :], window)
+                else:
                     nc.scalar.activation(hid_planes[g][:, t, :], window, ACT.Copy)
 
-        groups = []
+        fronts = [front(t) for t in range(2)]
+        late = None
+        for t in range(PACK):
+            if t + 2 < PACK:
+                fronts.append(front(t + 2))
+            late = middle(t, *fronts[t], late)
+        look_up_genes(PACK - 1)
+
         for g in range(2):
             grouped = work.tile([P, GH, PACK], BF16, name="grouped", align_bytes=64)
             nc.vector.tensor_copy(
-                out=grouped[:, :, : PACK - 1].rearrange("p (c i) t -> p c t i", i=4),
-                in_=hid_planes[g][:, : PACK - 1, :].rearrange("p t (c i) -> p c t i", i=4),
-            )
-            groups.append(grouped)
-        for g in range(2):
-            grouped = groups[g]
-            nc.vector.tensor_copy(
-                grouped[:, :, PACK - 1], enh[PACK - 1][:].indirect(gene_t[:, g * (GH // 16) : (g + 1) * (GH // 16)])
+                out=grouped[:].rearrange("p (c i) t -> p c t i", i=4),
+                in_=hid_planes[g][:].rearrange("p t (c i) -> p c t i", i=4),
             )
             codes = work.tile([P, GH], U32, name="codes", align_bytes=64)
             scales = work.tile([P, GH], U8, name="scales", align_bytes=64)

@@ -149,23 +149,25 @@ def tile_picked_ytfcmp_sig_p_kernel(
                 kd.append(kd_h)
             return z, kd, picked
 
-        def middle(t, z, kd, picked, late):
-            part = psum.tile([P, V], F32, name="part", tag="part", bufs=1)
-            wt = []
-            for h in range(2):
-                cc = work.tile([P, HALF], F32, name="cc", tag="cc", bufs=2)
-                nc.vector.scalar_tensor_tensor(
-                    cc[:], picked[h][:], 5.0 / 3.0, conc_t[t][:, h * HALF : (h + 1) * HALF], ALU.add, ALU.mult
-                )
-                wt_h = work.tile([P, HALF], F32, name="wt_h", tag="wt_h", bufs=4)
-                nc.vector.tensor_tensor(as_pairs(wt_h[:]), paired(cc[:]), as_pairs(kd[h][:]), ALU.mult)
-                wt.append(wt_h)
-                group_sums(part[:, h * P : (h + 1) * P], wt_h, [])
+        def weigh(t, h, kd, picked, part):
+            cc = work.tile([P, HALF], F32, name="cc", tag="cc", bufs=2)
+            nc.vector.scalar_tensor_tensor(
+                cc[:], picked[h][:], 5.0 / 3.0, conc_t[t][:, h * HALF : (h + 1) * HALF], ALU.add, ALU.mult
+            )
+            wt_h = work.tile([P, HALF], F32, name="wt_h", tag="wt_h", bufs=4)
+            nc.vector.tensor_tensor(as_pairs(wt_h[:]), paired(cc[:]), as_pairs(kd[h][:]), ALU.mult)
+            group_sums(part[:, h * P : (h + 1) * P], wt_h, [])
+            return wt_h
+
+        def drive(z, wt):
             num = psum.tile([P, V], F32, name="num", tag="num", bufs=1)
             for h in range(2):
                 wz = work.tile([P, HALF], F32, name="wz", tag="wz", bufs=2)
                 nc.vector.tensor_tensor(as_pairs(wz[:]), paired(z[h][:]), as_pairs(wt[h][:]), ALU.mult)
                 group_sums(num[:, (1 - h) * P : (2 - h) * P], wz, [])
+            return num
+
+        def middle(t, part, num, late):
             part_sb = enh[t][:, V:]
             nc.vector.tensor_scalar(part_sb, part[:], 0.375 * SHRINK, 0.5 * SHRINK, ALU.mult, ALU.add)
             prod = work.tile([P, 1, P], F32, name="prod")
@@ -182,7 +184,7 @@ def tile_picked_ytfcmp_sig_p_kernel(
             )
             if t == PACK - 1:
                 pu = work.tile([P, V], F32, name="pu")
-                turn(pu[:], [part_sb[:, h * P : (h + 1) * P] for h in range(2)], "part", ACT.Copy, unit_s[:, t : t + 1])
+                turn(pu[:], [part_sb[:, h * P : (h + 1) * P] for h in range(2)], "y", ACT.Copy, unit_s[:, t : t + 1])
                 td = work.tile([P, V], F32, name="td")
                 turn(td[:], [drv[:, 1 - h, :] for h in range(2)], "num", ACT.Tanh, 0.375 * SHRINK)
                 nc.vector.scalar_tensor_tensor(enh[t][:, :V], td[:], 1.0, pu[:], ALU.add, ALU.mult)
@@ -193,7 +195,7 @@ def tile_picked_ytfcmp_sig_p_kernel(
             return t, td
 
         def turn(dst, halves, tag, func, scale):
-            back = psum.tile([P, V], F32, name="back", tag=tag, bufs=1)
+            back = psum.tile([P, V], F32, name="back", tag=tag, bufs=2 if tag == "y" else 1)
             for h in range(2):
                 nc.tensor.transpose(back[:, h * P : (h + 1) * P], halves[h], ident[:])
             nc.scalar.activation(dst, back[:], func, scale=scale)
@@ -201,7 +203,7 @@ def tile_picked_ytfcmp_sig_p_kernel(
         def finish(t, td):
             ft = work.tile([P, V], F32, name="ft")
             nc.vector.scalar_tensor_tensor(ft[:], td[:], 1.0, enh[t][:, V:], ALU.add, ALU.mult)
-            turn(enh[t][:, :V], [ft[:, h * P : (h + 1) * P] for h in range(2)], "part", ACT.Copy, unit_s[:, t : t + 1])
+            turn(enh[t][:, :V], [ft[:, h * P : (h + 1) * P] for h in range(2)], "y", ACT.Copy, unit_s[:, t : t + 1])
             look_up_genes(t)
 
         def look_up_genes(t):
@@ -213,16 +215,23 @@ def tile_picked_ytfcmp_sig_p_kernel(
                     nc.scalar.activation(hid_planes[g][:, t, :], window, ACT.Copy)
 
         fronts = [front(t) for t in range(2)]
-        late = None
+        late = sums = None
         for t in range(PACK):
             if t + 2 < PACK:
                 fronts.append(front(t + 2))
-            late = middle(t, *fronts[t], late)
+            z, kd, picked = fronts[t]
+            part = psum.tile([P, V], F32, name="part", tag="part", bufs=1)
+            wt = [weigh(t, 0, kd, picked, part)]
+            wt.append(weigh(t, 1, kd, picked, part))
+            if sums:
+                late = middle(t - 1, *sums, late)
+            sums = (part, drive(z, wt))
+        middle(PACK - 1, *sums, late)
         look_up_genes(PACK - 1)
 
         for g in range(2):
             grouped = work.tile([P, GH, PACK], BF16, name="grouped", align_bytes=64)
-            nc.vector.tensor_copy(
+            (nc.vector.tensor_copy if g == 0 else nc.scalar.copy)(
                 out=grouped[:].rearrange("p (c i) t -> p c t i", i=4),
                 in_=hid_planes[g][:].rearrange("p t (c i) -> p c t i", i=4),
             )
@@ -241,7 +250,7 @@ def tile_picked_ytfcmp_sig_p_kernel(
                     stop=True,
                 )
                 res = work.tile([P, GH], F32, name="res", tag="res", bufs=4)
-                if g == 1 and m == 1:
+                if (g + m) % 2 == 0:
                     nc.vector.tensor_copy(res[:], acc[:])
                 else:
                     nc.scalar.copy(res[:], acc[:])

@@ -22,7 +22,7 @@ PACK = 4
 HALF = 512
 LIST_COLS = HALF // 16
 GH = U // 2
-SHRINK = 2.0**-48
+SHRINK = 2.0**-64
 
 
 def load_scale_rows(queue, plane, scales, quads=range(4)):
@@ -100,7 +100,7 @@ def tile_picked_ytfcmp_sig_p_kernel(
             nc.vector.tensor_copy(xw[h][:], x_tab[:].indirect(offs_t[:, h * LIST_COLS : (h + 1) * LIST_COLS]))
 
         make_identity(nc, ident[:])
-        nc.gpsimd.tensor_scalar(unit_s[:], unit_t[:], 1.0 / SHRINK, 0.0, ALU.mult, ALU.add)
+        nc.gpsimd.tensor_scalar(unit_s[:], unit_t[:], 0.375 / SHRINK, 0.0, ALU.mult, ALU.add)
 
         def product(acc, i, t, h):
             nc.tensor.matmul_mx(
@@ -124,6 +124,8 @@ def tile_picked_ytfcmp_sig_p_kernel(
             for n, member in enumerate(members):
                 nc.tensor.matmul(acc, member, ident[:], start=(n == 0), stop=(n == len(members) - 1), is_transpose=True)
 
+        cc_slots = [keep.tile([P, HALF], F32, name="cc%d" % h) for h in range(2)]
+
         def front(t):
             z = [psum.tile([P, HALF], F32, name="z%d" % h, tag="z", bufs=4) for h in range(2)]
             y = [psum.tile([P, HALF], F32, name="y%d" % h, tag="y", bufs=2) for h in range(2)]
@@ -139,7 +141,7 @@ def tile_picked_ytfcmp_sig_p_kernel(
                 if (t, h) in ((0,0),(0,1)):
                     nc.vector.tensor_copy(pick[:], window)
                 else:
-                    nc.scalar.activation(pick[:], window, ACT.Copy)
+                    nc.scalar.activation(pick[:], window, ACT.Copy, bias=5.0 / 3.0)
                 picked.append(pick)
             for h in range(2):
                 th = work.tile([P, HALF], F32, name="th", tag="th", bufs=2)
@@ -150,10 +152,13 @@ def tile_picked_ytfcmp_sig_p_kernel(
             return z, kd, picked
 
         def weigh(t, h, kd, picked, part):
-            cc = work.tile([P, HALF], F32, name="cc", tag="cc", bufs=2)
-            nc.vector.scalar_tensor_tensor(
-                cc[:], picked[h][:], 5.0 / 3.0, conc_t[t][:, h * HALF : (h + 1) * HALF], ALU.add, ALU.mult
-            )
+            cc = cc_slots[(t + h) % 2]
+            if (t, h) in ((0,0),(0,1)):
+                nc.vector.scalar_tensor_tensor(
+                    cc[:], picked[h][:], 5.0 / 3.0, conc_t[t][:, h * HALF : (h + 1) * HALF], ALU.add, ALU.mult
+                )
+            else:
+                (nc.vector if (t, h) in () else nc.gpsimd).tensor_tensor(cc[:], picked[h][:], conc_t[t][:, h * HALF : (h + 1) * HALF], ALU.mult)
             wt_h = work.tile([P, HALF], F32, name="wt_h", tag="wt_h", bufs=4)
             nc.vector.tensor_tensor(as_pairs(wt_h[:]), paired(cc[:]), as_pairs(kd[h][:]), ALU.mult)
             group_sums(part[:, h * P : (h + 1) * P], wt_h, [])
@@ -169,9 +174,9 @@ def tile_picked_ytfcmp_sig_p_kernel(
 
         def middle(t, part, num, late):
             part_sb = enh[t][:, V:]
-            nc.vector.tensor_scalar(part_sb, part[:], 0.375 * SHRINK, 0.5 * SHRINK, ALU.mult, ALU.add)
+            nc.vector.tensor_scalar(part_sb, part[:], 4.0 / 3.0, SHRINK, ALU.add, ALU.mult)
             prod = work.tile([P, 1, P], F32, name="prod")
-            nc.vector.tensor_tensor(prod[:, 0, :], part_sb[:, :P], part_sb[:, P:], ALU.mult)
+            nc.vector.scalar_tensor_tensor(prod[:, 0, :], part[:, P:], 4.0 / 3.0, part_sb[:, :P], ALU.add, ALU.mult)
             if late:
                 finish(*late)
             inv = work.tile([P, 1, P], F32, name="inv")
@@ -186,12 +191,12 @@ def tile_picked_ytfcmp_sig_p_kernel(
                 pu = work.tile([P, V], F32, name="pu")
                 turn(pu[:], [part_sb[:, h * P : (h + 1) * P] for h in range(2)], "y", ACT.Copy, unit_s[:, t : t + 1])
                 td = work.tile([P, V], F32, name="td")
-                turn(td[:], [drv[:, 1 - h, :] for h in range(2)], "num", ACT.Tanh, 0.375 * SHRINK)
+                turn(td[:], [drv[:, 1 - h, :] for h in range(2)], "num", ACT.Tanh, 1.0)
                 nc.vector.scalar_tensor_tensor(enh[t][:, :V], td[:], 1.0, pu[:], ALU.add, ALU.mult)
                 return None
             td = work.tile([P, V], F32, name="td")
             for h in range(2):
-                nc.scalar.activation(td[:, h * P : (h + 1) * P], drv[:, 1 - h, :], ACT.Tanh, scale=0.375 * SHRINK)
+                nc.scalar.activation(td[:, h * P : (h + 1) * P], drv[:, 1 - h, :], ACT.Tanh)
             return t, td
 
         def turn(dst, halves, tag, func, scale):

from contextlib import ExitStack

import concourse.mybir as mybir
from concourse.masks import make_identity

K, T, S, D, N, H, V, U = 512, 4096, 1024, 4, 256, 512, 256, 512
FLOPS = 2 * K * H * S * 2 + 2 * H * N * U

F32 = mybir.dt.float32
BF16 = mybir.dt.bfloat16
I32 = mybir.dt.int32
U32 = mybir.dt.uint32
U16 = mybir.dt.uint16
U8 = mybir.dt.uint8
FP8X4 = mybir.dt.float8_e4m3fn_x4
FP4X4 = mybir.dt.float4_e2m1fn_x4
ACT = mybir.ActivationFunctionType
ALU = mybir.AluOpType

P = 128
PACK = 4
HALF = 512
LIST_COLS = HALF // 16
GH = U // 2
SHRINK = 2.0**-64


def load_scale_rows(queue, plane, scales, quads=range(4)):
    for quad in quads:
        queue.dma_start(
            out=plane[32 * quad : 32 * quad + 4, :].bitcast(I32),
            in_=scales[0, 4 * quad : 4 * quad + 4, :].bitcast(I32),
        )


def tile_picked_ytfcmp_sig_p_kernel(
    tc, x_words, x_scales, w1_words, w1_scales, w2_words, w2_scales, conc, unit, w3_words, w3_scales, offs, cof, gene, out
):
    nc = tc.nc
    with ExitStack() as ctx:
        keep = ctx.enter_context(tc.tile_pool(name="keep", bufs=1))
        work = ctx.enter_context(tc.tile_pool(name="work", bufs=2))
        psum = ctx.enter_context(tc.psum_pool(name="psum", bufs=1))

        offs_t = keep.tile([P, S // 16], U16, name="offs_t")
        cof_t = keep.tile([P, S // 16], U16, name="cof_t")
        gene_t = keep.tile([P, U // 16], U16, name="gene_t")

        x_tab = keep.tile([P, T], U32, name="x_tab", align_bytes=64)
        xs_tab = keep.tile([P, T], U8, name="xs_tab", align_bytes=64)
        w_raw = [keep.tile([P, 2 * H], U8, name="w_raw%d" % i, align_bytes=64) for i in range(2)]
        ws_raw = [keep.tile([P, H], U8, name="ws_raw%d" % i, align_bytes=64) for i in range(2)]
        w_deal = [keep.tile([P, 2 * H], U8, name="w_deal%d" % i, align_bytes=64) for i in range(2)]
        ws_deal = [keep.tile([P, H], U8, name="ws_deal%d" % i, align_bytes=64) for i in range(2)]
        w3_t = keep.tile([P, 2 * N], U8, name="w3_t", align_bytes=64)
        w3s_t = keep.tile([P, N], U8, name="w3s_t", align_bytes=64)
        conc_t = [keep.tile([P, S], F32, name="conc%d" % t) for t in range(PACK)]
        unit_t = keep.tile([P, PACK], F32, name="unit_t")
        ident = keep.tile([P, P], F32, name="ident")
        unit_s = keep.tile([P, PACK], F32, name="unit_s")
        enh = [keep.tile([P, 2 * V], F32, name="enh%d" % t) for t in range(PACK)]
        hid_planes = [keep.tile([P, PACK, GH], BF16, name="hid_planes%d" % g, align_bytes=64) for g in range(2)]

        nc.vector.memset(xs_tab[:].bitcast(I32), 0)
        for i in range(2):
            nc.gpsimd.memset(ws_raw[i][:].bitcast(I32), 0)
        nc.sync.dma_start(offs_t[:], offs)
        load_scale_rows(nc.scalar, xs_tab, x_scales)
        nc.sync.dma_start(out=w_raw[0][:].bitcast(I32), in_=w2_words[0].bitcast(I32))
        nc.sync.dma_start(out=w_raw[1][:].bitcast(I32), in_=w1_words[0].bitcast(I32))
        load_scale_rows(nc.sync, ws_raw[0], w2_scales, range(1))
        nc.sync.dma_start(out=x_tab[:].bitcast(I32), in_=x_words[0].rearrange("p n t -> p (n t)").bitcast(I32))
        load_scale_rows(nc.scalar, ws_raw[0], w2_scales, range(1, 4))
        nc.sync.dma_start(cof_t[:], cof)
        load_scale_rows(nc.sync, ws_raw[1], w1_scales)
        conc_rows = conc.rearrange("(p t) s -> p t s", t=PACK)
        for t in range(PACK):
            nc.sync.dma_start(out=conc_t[t][:], in_=conc_rows[:, t, :])
        nc.sync.dma_start(gene_t[:], gene)
        nc.sync.dma_start(out=unit_t[:], in_=unit.rearrange("(p t) o -> p (t o)", t=PACK))
        nc.sync.dma_start(out=w3_t[:].bitcast(I32), in_=w3_words[0].bitcast(I32))
        nc.gpsimd.memset(w3s_t[:].bitcast(I32), 0)
        load_scale_rows(nc.sync, w3s_t, w3_scales)

        for i, eng in enumerate((nc.vector, nc.vector)):
            eng.tensor_copy(
                out=w_deal[i][:].rearrange("p (t m b) -> p t m b", t=PACK, b=2),
                in_=w_raw[i][:].rearrange("p (m t b) -> p t m b", t=PACK, b=2),
            )
        xw = [keep.tile([P, HALF], U32, name="xw%d" % h, align_bytes=64) for h in range(2)]
        xs = [keep.tile([P, HALF], U8, name="xs%d" % h, align_bytes=64) for h in range(2)]
        for h in range(2):
            nc.vector.tensor_copy(xs[h][:], xs_tab[:].indirect(offs_t[:, h * LIST_COLS : (h + 1) * LIST_COLS]))
        for i, eng in enumerate((nc.vector, nc.vector)):
            eng.tensor_copy(
                out=ws_deal[i][:].rearrange("p (t m) -> p t m", t=PACK),
                in_=ws_raw[i][:].rearrange("p (m t) -> p t m", t=PACK),
            )
        for h in range(2):
            nc.vector.tensor_copy(xw[h][:], x_tab[:].indirect(offs_t[:, h * LIST_COLS : (h + 1) * LIST_COLS]))

        make_identity(nc, ident[:])
        nc.gpsimd.tensor_scalar(unit_s[:], unit_t[:], 0.375 / SHRINK, 0.0, ALU.mult, ALU.add)

        def product(acc, i, t, h):
            nc.tensor.matmul_mx(
                out=acc[:],
                lhsT=w_deal[i][:, 2 * P * t : 2 * P * (t + 1)].bitcast(FP4X4),
                lhsT_scale=ws_deal[i][:, P * t : P * (t + 1)],
                rhs=xw[h][:].bitcast(FP8X4),
                rhs_scale=xs[h][:],
                start=True,
                stop=True,
            )

        def paired(ap):
            return ap.rearrange("p (v e b) -> p e v b", e=2, b=2)

        def as_pairs(ap):
            return ap.rearrange("p (e v b) -> p e v b", e=2, b=2)

        def group_sums(acc, values, first):
            members = first + [values[:, e * 256 + b : (e + 1) * 256 : 2] for e in range(2) for b in range(2)]
            for n, member in enumerate(members):
                nc.tensor.matmul(acc, member, ident[:], start=(n == 0), stop=(n == len(members) - 1), is_transpose=True)

        cc_slots = [keep.tile([P, HALF], F32, name="cc%d" % h) for h in range(2)]

        def front(t):
            z = [psum.tile([P, HALF], F32, name="z%d" % h, tag="z", bufs=4) for h in range(2)]
            y = [psum.tile([P, HALF], F32, name="y%d" % h, tag="y", bufs=2) for h in range(2)]
            tz = work.tile([P, S], F32, name="tz", tag="tz%d" % (t % 2), bufs=1)
            kd, picked = [], []
            for h in range(2):
                product(z[h], 0, t, h)
                product(y[h], 1, t, h)
                nc.scalar.activation(tz[:, h * HALF : (h + 1) * HALF], z[h][:], ACT.Tanh, scale=0.5)
            for h in range(2):
                pick = work.tile([P, HALF], F32, name="pick", tag="pick", bufs=6)
                window = tz[:].indirect(cof_t[:, h * LIST_COLS : (h + 1) * LIST_COLS])
                if (t, h) in ((0,0),(0,1)):
                    nc.vector.tensor_copy(pick[:], window)
                else:
                    nc.scalar.activation(pick[:], window, ACT.Copy, bias=5.0 / 3.0)
                picked.append(pick)
            for h in range(2):
                th = work.tile([P, HALF], F32, name="th", tag="th", bufs=2)
                nc.scalar.activation(as_pairs(th[:]), paired(y[h][:]), ACT.Tanh)
                kd_h = work.tile([P, HALF], F32, name="kd_h", tag="kd_h", bufs=6)
                nc.scalar.activation(kd_h[:], th[:], ACT.Exp)
                kd.append(kd_h)
            return z, kd, picked

        def weigh(t, h, kd, picked, part):
            cc = cc_slots[(t + h) % 2]
            if (t, h) in ((0,0),(0,1)):
                nc.vector.scalar_tensor_tensor(
                    cc[:], picked[h][:], 5.0 / 3.0, conc_t[t][:, h * HALF : (h + 1) * HALF], ALU.add, ALU.mult
                )
            else:
                (nc.vector if (t, h) in () else nc.gpsimd).tensor_tensor(cc[:], picked[h][:], conc_t[t][:, h * HALF : (h + 1) * HALF], ALU.mult)
            wt_h = work.tile([P, HALF], F32, name="wt_h", tag="wt_h", bufs=4)
            nc.vector.tensor_tensor(as_pairs(wt_h[:]), paired(cc[:]), as_pairs(kd[h][:]), ALU.mult)
            group_sums(part[:, h * P : (h + 1) * P], wt_h, [])
            return wt_h

        def drive(z, wt):
            num = psum.tile([P, V], F32, name="num", tag="num", bufs=1)
            for h in range(2):
                wz = work.tile([P, HALF], F32, name="wz", tag="wz", bufs=2)
                nc.vector.tensor_tensor(as_pairs(wz[:]), paired(z[h][:]), as_pairs(wt[h][:]), ALU.mult)
                group_sums(num[:, (1 - h) * P : (2 - h) * P], wz, [])
            return num

        def middle(t, part, num, late):
            part_sb = enh[t][:, V:]
            nc.vector.tensor_scalar(part_sb, part[:], 4.0 / 3.0, SHRINK, ALU.add, ALU.mult)
            prod = work.tile([P, 1, P], F32, name="prod")
            nc.vector.scalar_tensor_tensor(prod[:, 0, :], part[:, P:], 4.0 / 3.0, part_sb[:, :P], ALU.add, ALU.mult)
            if late:
                finish(*late)
            inv = work.tile([P, 1, P], F32, name="inv")
            nc.vector.reciprocal(inv[:], prod[:])
            cross = work.tile([P, V], F32, name="cross")
            nc.vector.tensor_tensor(cross[:], num[:], part_sb, ALU.mult)
            drv = work.tile([P, 2, P], F32, name="drv")
            nc.vector.tensor_tensor(
                drv[:], cross[:].rearrange("p (h v) -> p h v", h=2), inv[:].to_broadcast([P, 2, P]), ALU.mult
            )
            if t == PACK - 1:
                pu = work.tile([P, V], F32, name="pu")
                turn(pu[:], [part_sb[:, h * P : (h + 1) * P] for h in range(2)], "y", ACT.Copy, unit_s[:, t : t + 1])
                td = work.tile([P, V], F32, name="td")
                turn(td[:], [drv[:, 1 - h, :] for h in range(2)], "num", ACT.Tanh, 1.0)
                nc.vector.scalar_tensor_tensor(enh[t][:, :V], td[:], 1.0, pu[:], ALU.add, ALU.mult)
                return None
            td = work.tile([P, V], F32, name="td")
            for h in range(2):
                nc.scalar.activation(td[:, h * P : (h + 1) * P], drv[:, 1 - h, :], ACT.Tanh)
            return t, td

        def turn(dst, halves, tag, func, scale):
            back = psum.tile([P, V], F32, name="back", tag=tag, bufs=2 if tag == "y" else 1)
            for h in range(2):
                nc.tensor.transpose(back[:, h * P : (h + 1) * P], halves[h], ident[:])
            nc.scalar.activation(dst, back[:], func, scale=scale)

        def finish(t, td):
            ft = work.tile([P, V], F32, name="ft")
            nc.vector.scalar_tensor_tensor(ft[:], td[:], 1.0, enh[t][:, V:], ALU.add, ALU.mult)
            turn(enh[t][:, :V], [ft[:, h * P : (h + 1) * P] for h in range(2)], "y", ACT.Copy, unit_s[:, t : t + 1])
            look_up_genes(t)

        def look_up_genes(t):
            for g in range(2):
                window = enh[t][:].indirect(gene_t[:, g * (GH // 16) : (g + 1) * (GH // 16)])
                if t == PACK - 1 and g == 0:
                    nc.vector.tensor_copy(hid_planes[g][:, t, :], window)
                else:
                    nc.scalar.activation(hid_planes[g][:, t, :], window, ACT.Copy)

        fronts = [front(t) for t in range(2)]
        late = sums = None
        for t in range(PACK):
            if t + 2 < PACK:
                fronts.append(front(t + 2))
            z, kd, picked = fronts[t]
            part = psum.tile([P, V], F32, name="part", tag="part", bufs=1)
            wt = [weigh(t, 0, kd, picked, part)]
            wt.append(weigh(t, 1, kd, picked, part))
            if sums:
                late = middle(t - 1, *sums, late)
            sums = (part, drive(z, wt))
        middle(PACK - 1, *sums, late)
        look_up_genes(PACK - 1)

        for g in range(2):
            grouped = work.tile([P, GH, PACK], BF16, name="grouped", align_bytes=64)
            (nc.vector.tensor_copy if g == 0 else nc.scalar.copy)(
                out=grouped[:].rearrange("p (c i) t -> p c t i", i=4),
                in_=hid_planes[g][:].rearrange("p t (c i) -> p c t i", i=4),
            )
            codes = work.tile([P, GH], U32, name="codes", align_bytes=64)
            scales = work.tile([P, GH], U8, name="scales", align_bytes=64)
            nc.vector.quantize_mx(out=codes[:].bitcast(FP8X4), scales=scales[:], in_=grouped[:].rearrange("p r t -> p (r t)"))
            for m in range(N // P):
                acc = psum.tile([P, GH], F32, name="acc", tag="z", bufs=4)
                nc.tensor.matmul_mx(
                    out=acc[:],
                    lhsT=w3_t[:, 2 * P * m : 2 * P * (m + 1)].bitcast(FP4X4),
                    lhsT_scale=w3s_t[:, P * m : P * (m + 1)],
                    rhs=codes[:].bitcast(FP8X4),
                    rhs_scale=scales[:],
                    start=True,
                    stop=True,
                )
                res = work.tile([P, GH], F32, name="res", tag="res", bufs=4)
                if (g + m) % 2 == 0:
                    nc.vector.tensor_copy(res[:], acc[:])
                else:
                    nc.scalar.copy(res[:], acc[:])
                nc.sync.dma_start(out=out[m * P : (m + 1) * P, g * GH : (g + 1) * GH], in_=res[:])
